import numpy as np
import ml_dtypes


def mxq(x, axis, fmt="e4m3"):
    dtype, down = {"e4m3": (ml_dtypes.float8_e4m3fn, 7), "e5m2": (ml_dtypes.float8_e5m2, 14)}[fmt]
    v = np.moveaxis(np.asarray(x, np.float32).astype(ml_dtypes.bfloat16).astype(np.float64), axis, -1)
    blocks = v.reshape(v.shape[:-1] + (-1, 32))
    amax = np.abs(blocks).max(-1, keepdims=True)
    byte = np.maximum(np.where(amax > 0, np.frexp(amax)[1] - 1 + 127, 0) - down, 1)
    scale = np.exp2(byte - 127.0)
    codes = (blocks / scale).astype(np.float32).astype(dtype).astype(np.float64)
    return np.moveaxis((codes * scale).reshape(v.shape), -1, axis)


WIDE = False


def mx_kscale(k):
    if not WIDE:
        return np.ones(k)
    levels = np.array([10, -10, 5, -5, 0])
    if k % 512:
        return np.exp2(np.random.permutation(np.resize(levels, k // 32))).repeat(32)
    a = np.empty((k // 512, 16))
    for p in range(k // 512):
        a[p, :8] = np.random.permutation(np.resize(levels, 8))
        for g in range(8):
            far = levels[np.abs(levels - a[p, g]) >= 10]
            a[p, g + 8] = far[np.random.randint(len(far))]
    return np.exp2(a.ravel()).repeat(32)


def f64(x):
    return np.asarray(x).astype(np.float64)


def striped(idx):
    return np.tile(idx.reshape(-1, 16).T, (8, 1)).astype(np.uint16)


def unstriped(offs):
    return offs[:16].T.reshape(-1).astype(np.int64)


def pack_weight(w):
    k, n = w.shape
    w = f64(np.asarray(w, np.float32).astype(ml_dtypes.bfloat16)).reshape(k // 32, 32, n)
    amax = np.abs(w).max(1)
    byte = np.clip(np.where(amax > 0, np.frexp(amax)[1] - 1 + 127 - 7, 1), 1, 254)
    scaled = (w * np.exp2(127.0 - byte)[:, None, :]).reshape(k, n).astype(np.float32)
    words = np.ascontiguousarray(scaled.reshape(k // 512, 128, 4, n).transpose(0, 1, 3, 2)).astype(ml_dtypes.float8_e4m3fn).view(np.uint8)
    return words, np.ascontiguousarray(byte.astype(np.uint8).reshape(k // 512, 16, n))


def unpack_weight(words, scales):
    g, p, n, _ = words.shape
    vals = np.ascontiguousarray(words).view(ml_dtypes.float8_e4m3fn).astype(np.float64) * np.repeat(np.exp2(scales.astype(np.float64) - 127.0), 8, axis=1)[..., None]
    return vals.transpose(0, 1, 3, 2).reshape(g * 512, n)


def planes(y):
    n, m = y.shape
    v = y.astype(np.float32).astype(ml_dtypes.bfloat16).astype(np.float64).reshape(n // 32, 32, m)
    top = np.abs(v).max(1)
    byte = np.clip(np.where(top > 0, np.frexp(top)[1] - 1 + 127 - 7, 1), 1, 254)
    codes = (v * np.exp2(127.0 - byte)[:, None, :]).reshape(n, m).astype(np.float32).astype(ml_dtypes.float8_e4m3fn).view(np.uint8)
    words = codes.reshape(n // 512, 128, 4, m).transpose(0, 1, 3, 2)
    return np.ascontiguousarray(words), np.ascontiguousarray(byte.astype(np.uint8).reshape(n // 512, 16, m))


def sigmoid(v):
    return 1.0 / (1.0 + np.exp(-np.maximum(v, -700.0)))


K, T, S, V, H, N = 512, 1024, 512, 256, 512, 512


def setup_inputs():
    n = np.random.standard_normal
    s = mx_kscale(K)[:, None]
    u = mx_kscale(H)
    near = np.random.permutation(S)
    packed_xT = pack_weight(n((K, T)) * s)
    return {
        "x_words": packed_xT[0],
        "x_scales": packed_xT[1],
        "w1": (n((K, N)) / np.sqrt(K) / s).astype(np.float32),
        "w2": (n((K, H)) / np.sqrt(K) / s * u).astype(np.float32),
        "w3": (n((K, N)) / np.sqrt(K) / s).astype(np.float32),
        "w4": (n((H, N)) / np.sqrt(H) / u[:, None]).astype(np.float32),
        "w5": (n((K, N)) / np.sqrt(K) / s).astype(np.float32),
        "offs": striped(np.random.permutation(T)[:S]),
        "pos1": striped(near[:V]),
        "pos2": striped(near[V:]),
        "pos3": striped(np.random.permutation(S)[:V]),
        "nxt1": striped(np.random.permutation(S)[:V]),
        "nxt2": striped(np.random.permutation(S)[:V]),
        "nxt3": striped(np.random.permutation(S)[:V]),
        "own": striped(np.random.permutation(S)[:V]),
    }


def reference(x_words, x_scales, w1, w2, w3, w4, w5, offs, pos1, pos2, pos3, nxt1, nxt2, nxt3, own):
    xq = unpack_weight(x_words, x_scales)[:, unstriped(offs)]
    gg = sigmoid(mxq(f64(w5), 0, "e4m3").T @ xq)
    y = mxq(f64(w2), 0, "e4m3").T @ xq
    a = (sigmoid(mxq(f64(w1), 0, "e4m3").T @ xq)) * y
    ap0 = a[:, unstriped(pos1)]
    ee = mxq(f64(w3), 0, "e4m3").T @ xq
    ap1 = a[:, unstriped(pos2)]
    ap2 = a[:, unstriped(pos3)]
    z = ap0 * ee[:, unstriped(nxt1)] + ap1 * ee[:, unstriped(nxt2)] + ap2 * ee[:, unstriped(nxt3)]
    rr = mxq(f64(w4), 0, "e4m3").T @ mxq(z, 0, "e4m3")
    out_0 = gg[:, unstriped(own)] * rr
    return (out_0,) + planes(out_0)

@@ -1,0 +1,180 @@
+from contextlib import ExitStack
+
+import concourse.mybir as mybir
+
+F32 = mybir.dt.float32
+BF16 = mybir.dt.bfloat16
+I32 = mybir.dt.int32
+U32 = mybir.dt.uint32
+U16 = mybir.dt.uint16
+U8 = mybir.dt.uint8
+FP8X4 = mybir.dt.float8_e4m3fn_x4
+MULT = mybir.AluOpType.mult
+ADD = mybir.AluOpType.add
+SIGMOID = mybir.ActivationFunctionType.Sigmoid
+
+P = 128
+PACK = 4
+T, S, V, C = 1024, 512, 256, 512
+HALF = V // 2
+FLOPS = 1207959552
+
+
+def tile_picked_ytri_gated_po_kernel(
+    tc, x_words, x_scales, w1, w2, w3, w4, w5, offs, pos1, pos2, pos3, nxt1, nxt2, nxt3, own, out_0, out_1, out_2
+):
+    nc = tc.nc
+    with ExitStack() as ctx:
+        keep = ctx.enter_context(tc.tile_pool(name="keep", bufs=1))
+        psum = ctx.enter_context(tc.psum_pool(name="psum", bufs=8))
+
+        def load_list(name, src):
+            tile = keep.tile(list(src.shape), U16, name=name)
+            nc.sync.dma_start(tile[:], src)
+            return tile
+
+        def load_weight(name, src):
+            raw = keep.tile([P, PACK, C], F32, name=name)
+            nc.sync.dma_start(raw[:], src.rearrange("(p j) c -> p j c", j=PACK))
+            return raw
+
+        table_scales = keep.tile([P, T], U8, name="table_scales", align_bytes=64)
+        for q in range(4):
+            rows = x_scales[0, 4 * q : 4 * q + 4, :].bitcast(I32).rearrange("r c -> (r c)")
+            nc.scalar.dma_start(table_scales[32 * q : 32 * q + 32, :].bitcast(I32), rows.partition_broadcast(8))
+        offs_t = load_list("offs_t", offs)
+        table_words = keep.tile([P, T], I32, name="table_words", align_bytes=64)
+        nc.sync.dma_start(table_words[:], x_words[0].rearrange("p n t -> p (n t)").bitcast(I32))
+        raw3 = load_weight("raw3", w3)
+        nxt = [load_list("nxt%d_t" % d, src) for d, src in enumerate((nxt1, nxt2, nxt3))]
+        raw1 = load_weight("raw1", w1)
+        raw2 = load_weight("raw2", w2)
+        pos = [load_list("pos%d_t" % d, src) for d, src in enumerate((pos1, pos2, pos3))]
+        raw5 = load_weight("raw5", w5)
+        own_t = load_list("own_t", own)
+        raw4 = load_weight("raw4", w4)
+
+        x_codes = keep.tile([P, S], I32, name="x_codes", align_bytes=64)
+        x_plane = keep.tile([P, S], U8, name="x_plane", align_bytes=64)
+        nc.vector.tensor_copy(x_codes[:].bitcast(U32), table_words[:].bitcast(U32).indirect(offs_t[:]))
+        nc.vector.tensor_copy(x_plane[:], table_scales[:].indirect(offs_t[:]))
+
+        def round_weight(name, raw, scalar_share):
+            grouped = keep.tile([P, PACK * C], BF16, name=name, align_bytes=64)
+            dst = grouped[:].rearrange("p (t m j) -> p m j t", t=PACK, j=PACK)
+            src = raw[:].rearrange("p j (m t) -> p m j t", t=PACK)
+            nc.scalar.copy(dst[:, :scalar_share], src[:, :scalar_share])
+            if scalar_share < P:
+                nc.vector.tensor_copy(dst[:, scalar_share:], src[:, scalar_share:])
+            return grouped
+
+        def quantise(name, grouped, pieces):
+            width = grouped.shape[1] // PACK
+            codes = keep.tile([P, width], U32, name=name + "_codes", align_bytes=64)
+            plane = keep.tile([P, width], U8, name=name + "_plane", align_bytes=64)
+            for lo, hi in pieces:
+                nc.vector.quantize_mx(
+                    out=codes[:, lo:hi].bitcast(FP8X4), scales=plane[:, lo:hi], in_=grouped[:, PACK * lo : PACK * hi]
+                )
+            return codes, plane
+
+        def product(out, weight, t, codes, plane):
+            cols = slice(t * P, (t + 1) * P)
+            nc.tensor.matmul_mx(
+                out=out,
+                lhsT=weight[0][:, cols].bitcast(FP8X4),
+                lhsT_scale=weight[1][:, cols],
+                rhs=codes.bitcast(FP8X4),
+                rhs_scale=plane,
+                start=True,
+                stop=True,
+            )
+
+        def edge_product(weight, t):
+            acc = psum.tile([P, S], F32, name="acc")
+            product(acc[:], weight, t, x_codes[:], x_plane[:])
+            return acc
+
+        whole = [(0, C)]
+        q3 = quantise("q3", round_weight("g3", raw3, 44), [(0, 128), (128, 256), (256, 512)])
+
+        picked_ee = []
+
+        def ee_stage(t):
+            acc = edge_product(q3, t)
+            ee = keep.tile([P, S], F32, name="ee%d" % t)
+            nc.scalar.copy(ee[:], acc[:])
+            picked = keep.tile([P, 3, V], F32, name="picked_ee%d" % t)
+            for d in range(3):
+                nc.vector.tensor_copy(picked[:, d, :], ee[:].indirect(nxt[d][:]))
+            picked_ee.append(picked)
+
+        ee_stage(0)
+        ee_stage(1)
+        q1 = quantise("q1", round_weight("g1", raw1, P), whole)
+        ee_stage(2)
+        q2 = quantise("q2", round_weight("g2", raw2, P), whole)
+        ee_stage(3)
+
+        pair_sum = keep.tile([P, PACK, V], F32, name="pair_sum")
+        third = keep.tile([P, PACK, V], F32, name="third")
+
+        def a_stage(t):
+            acc1 = edge_product(q1, t)
+            acc2 = edge_product(q2, t)
+            gate = keep.tile([P, S], F32, name="gate%d" % t)
+            nc.scalar.activation(gate[:], acc1[:], SIGMOID)
+            a = keep.tile([P, S], F32, name="a%d" % t)
+            nc.vector.tensor_tensor(a[:], acc2[:], gate[:], MULT)
+            terms = keep.tile([P, 2, V], F32, name="terms%d" % t)
+            for d in range(3):
+                dst = terms[:, d, :] if d < 2 else third[:, t, :]
+                nc.vector.tensor_tensor(dst, a[:].indirect(pos[d][:]), picked_ee[t][:, d, :], MULT)
+            nc.vector.tensor_tensor(pair_sum[:, t, :], terms[:, 0, :], terms[:, 1, :], ADD)
+
+        a_stage(0)
+        q5 = quantise("q5", round_weight("g5", raw5, P), whole)
+        a_stage(1)
+        q4 = quantise("q4", round_weight("g4", raw4, P), whole)
+        a_stage(2)
+        a_stage(3)
+
+        picked_gg = keep.tile([P, PACK, V], F32, name="picked_gg")
+        for t in range(PACK):
+            acc = edge_product(q5, t)
+            logits = keep.tile([P, S], F32, name="logits%d" % t)
+            nc.scalar.copy(logits[:], acc[:])
+            nc.scalar.activation(picked_gg[:, t, :], logits[:].indirect(own_t[:]), SIGMOID)
+
+        def by_lines(ap, h):
+            return ap[:, :, h * HALF : (h + 1) * HALF].rearrange("p t (c i) -> p c t i", i=4)
+
+        def interleaved(ap):
+            return ap.rearrange("p (c i t) -> p c t i", i=4, t=PACK)
+
+        z_grouped = [keep.tile([P, PACK * HALF], BF16, name="z_grouped%d" % h, align_bytes=64) for h in range(2)]
+        for h in range(2):
+            nc.vector.tensor_tensor(interleaved(z_grouped[h][:]), by_lines(pair_sum[:], h), by_lines(third[:], h), ADD)
+        qz = [quantise("qz%d" % h, z_grouped[h], [(0, HALF)]) for h in range(2)]
+
+        result = keep.tile([P, 2, PACK, HALF], F32, name="result")
+        out_grouped = keep.tile([P, PACK * V], BF16, name="out_grouped", align_bytes=64)
+        out_rows = out_0.rearrange("(p t) v -> p t v", t=PACK)
+        for h in range(2):
+            cols = slice(h * HALF, (h + 1) * HALF)
+            rr = psum.tile([P, S], F32, name="acc")
+            for t in range(PACK):
+                product(rr[:, t * HALF : (t + 1) * HALF], q4, t, qz[h][0][:], qz[h][1][:])
+            nc.vector.tensor_tensor(
+                result[:, h], rr[:].rearrange("p (t v) -> p t v", t=PACK), picked_gg[:, :, cols], MULT
+            )
+            nc.sync.dma_start(out_rows[:, :, cols], result[:, h])
+            nc.scalar.copy(
+                interleaved(out_grouped[:, h * PACK * HALF : (h + 1) * PACK * HALF]),
+                result[:, h].rearrange("p t (c i) -> p c t i", i=4),
+            )
+        out_codes, out_plane = quantise("qo", out_grouped, [(0, HALF), (HALF, V)])
+        nc.sync.dma_start(out_1[0].rearrange("p n t -> p (n t)").bitcast(I32), out_codes[:].bitcast(I32))
+        for q in range(4):
+            queue = nc.scalar if q % 2 else nc.sync
+            queue.dma_start(out_2[0, 4 * q : 4 * q + 4, :].bitcast(I32), out_plane[32 * q : 32 * q + 4, :].bitcast(I32))

@@ -1,6 +1,7 @@
 from contextlib import ExitStack
 
 import concourse.mybir as mybir
+from concourse.masks import make_identity
 
 F32 = mybir.dt.float32
 BF16 = mybir.dt.bfloat16
@@ -10,7 +11,6 @@ U16 = mybir.dt.uint16
 U8 = mybir.dt.uint8
 FP8X4 = mybir.dt.float8_e4m3fn_x4
 MULT = mybir.AluOpType.mult
-ADD = mybir.AluOpType.add
 SIGMOID = mybir.ActivationFunctionType.Sigmoid
 
 P = 128
@@ -26,155 +26,222 @@ def tile_picked_ytri_gated_po_kernel(
     nc = tc.nc
     with ExitStack() as ctx:
         keep = ctx.enter_context(tc.tile_pool(name="keep", bufs=1))
-        psum = ctx.enter_context(tc.psum_pool(name="psum", bufs=8))
+        shared = ctx.enter_context(tc.tile_pool(name="shared", bufs=1))
+        psum = ctx.enter_context(tc.psum_pool(name="psum", bufs=1))
+
+        def bank(n, shape):
+            return psum.tile(shape, F32, name="acc", tag="bank%d" % n)
 
         def load_list(name, src):
             tile = keep.tile(list(src.shape), U16, name=name)
             nc.sync.dma_start(tile[:], src)
             return tile
 
-        def load_weight(name, src):
-            raw = keep.tile([P, PACK, C], F32, name=name)
-            nc.sync.dma_start(raw[:], src.rearrange("(p j) c -> p j c", j=PACK))
+        def load_weight(name, src, lo, hi):
+            raw = keep.tile([P, PACK, hi - lo], F32, name=name)
+            nc.sync.dma_start(raw[:], src.rearrange("(p j) c -> p j c", j=PACK)[:, :, lo:hi])
             return raw
 
         table_scales = keep.tile([P, T], U8, name="table_scales", align_bytes=64)
         for q in range(4):
             rows = x_scales[0, 4 * q : 4 * q + 4, :].bitcast(I32).rearrange("r c -> (r c)")
             nc.scalar.dma_start(table_scales[32 * q : 32 * q + 32, :].bitcast(I32), rows.partition_broadcast(8))
+        warm = keep.tile([P, 2], F32, name="warm")
+        nc.gpsimd.memset(warm[:, 0:1], 0.0)
+        nc.scalar.activation(warm[:, 1:2], warm[:, 0:1], SIGMOID)
+
         offs_t = load_list("offs_t", offs)
         table_words = keep.tile([P, T], I32, name="table_words", align_bytes=64)
         nc.sync.dma_start(table_words[:], x_words[0].rearrange("p n t -> p (n t)").bitcast(I32))
-        raw3 = load_weight("raw3", w3)
+        raw3 = [load_weight("raw3_%d" % lo, w3, lo, hi) for lo, hi in ((0, 128), (128, 256), (256, 512))]
         nxt = [load_list("nxt%d_t" % d, src) for d, src in enumerate((nxt1, nxt2, nxt3))]
-        raw1 = load_weight("raw1", w1)
-        raw2 = load_weight("raw2", w2)
+        raw1_lo = load_weight("raw1_lo", w1, 0, V)
+        raw2_lo = load_weight("raw2_lo", w2, 0, V)
         pos = [load_list("pos%d_t" % d, src) for d, src in enumerate((pos1, pos2, pos3))]
-        raw5 = load_weight("raw5", w5)
+        raw1_hi = load_weight("raw1_hi", w1, V, C)
+        raw2_hi = load_weight("raw2_hi", w2, V, C)
+        raw5 = load_weight("raw5", w5, 0, C)
         own_t = load_list("own_t", own)
-        raw4 = load_weight("raw4", w4)
+        raw4 = shared.tile([P, PACK, C], F32, name="raw4", offset=0)
+        nc.sync.dma_start(raw4[:], w4.rearrange("(p j) c -> p j c", j=PACK))
+
+        identity = keep.tile([P, P], F32, name="identity")
+        make_identity(nc, identity[:])
 
         x_codes = keep.tile([P, S], I32, name="x_codes", align_bytes=64)
         x_plane = keep.tile([P, S], U8, name="x_plane", align_bytes=64)
-        nc.vector.tensor_copy(x_codes[:].bitcast(U32), table_words[:].bitcast(U32).indirect(offs_t[:]))
         nc.vector.tensor_copy(x_plane[:], table_scales[:].indirect(offs_t[:]))
+        nc.vector.tensor_copy(x_codes[:].bitcast(U32), table_words[:].bitcast(U32).indirect(offs_t[:]))
 
-        def round_weight(name, raw, scalar_share):
-            grouped = keep.tile([P, PACK * C], BF16, name=name, align_bytes=64)
-            dst = grouped[:].rearrange("p (t m j) -> p m j t", t=PACK, j=PACK)
-            src = raw[:].rearrange("p j (m t) -> p m j t", t=PACK)
-            nc.scalar.copy(dst[:, :scalar_share], src[:, :scalar_share])
-            if scalar_share < P:
-                nc.vector.tensor_copy(dst[:, scalar_share:], src[:, scalar_share:])
-            return grouped
+        def by_lines(ap):
+            return ap.rearrange("p t (c i) -> p c t i", i=4)
 
-        def quantise(name, grouped, pieces):
+        def interleaved(ap):
+            return ap.rearrange("p (c i t) -> p c t i", i=4, t=PACK)
+
+        def quantise(name, grouped):
             width = grouped.shape[1] // PACK
             codes = keep.tile([P, width], U32, name=name + "_codes", align_bytes=64)
             plane = keep.tile([P, width], U8, name=name + "_plane", align_bytes=64)
-            for lo, hi in pieces:
-                nc.vector.quantize_mx(
-                    out=codes[:, lo:hi].bitcast(FP8X4), scales=plane[:, lo:hi], in_=grouped[:, PACK * lo : PACK * hi]
-                )
+            nc.vector.quantize_mx(out=codes[:].bitcast(FP8X4), scales=plane[:], in_=grouped)
             return codes, plane
 
-        def product(out, weight, t, codes, plane):
-            cols = slice(t * P, (t + 1) * P)
+        def prepare_plain(name, raw):
+            grouped = keep.tile([P, PACK * raw.shape[2]], BF16, name=name, align_bytes=64)
+            nc.scalar.copy(interleaved(grouped[:]), by_lines(raw))
+            codes, plane = quantise(name, grouped[:])
+            return [(codes[:, lo : lo + P], plane[:, lo : lo + P]) for lo in range(0, raw.shape[2], P)]
+
+        def prepare_dealt(name, raws):
+            grouped = keep.tile([P, PACK * C], BF16, name=name, align_bytes=64)
+            dealt = grouped[:].rearrange("p (t m j) -> p m j t", t=PACK, j=PACK)
+            done = 0
+            for raw in raws:
+                count = raw.shape[2] // PACK
+                nc.scalar.copy(dealt[:, done : done + count], raw[:].rearrange("p j (m t) -> p m j t", t=PACK))
+                done = done + count
+            return grouped
+
+        def quantise_tiles(name, grouped):
+            codes, plane = quantise(name, grouped[:])
+            return [(codes[:, lo : lo + P], plane[:, lo : lo + P]) for lo in range(0, codes.shape[1], P)]
+
+        def product(out, weight, codes, plane):
             nc.tensor.matmul_mx(
                 out=out,
-                lhsT=weight[0][:, cols].bitcast(FP8X4),
-                lhsT_scale=weight[1][:, cols],
+                lhsT=weight[0].bitcast(FP8X4),
+                lhsT_scale=weight[1],
                 rhs=codes.bitcast(FP8X4),
                 rhs_scale=plane,
                 start=True,
                 stop=True,
             )
 
-        def edge_product(weight, t):
-            acc = psum.tile([P, S], F32, name="acc")
-            product(acc[:], weight, t, x_codes[:], x_plane[:])
+        def edge_product(weight, n):
+            acc = bank(n, [P, S])
+            product(acc[:], weight, x_codes[:], x_plane[:])
             return acc
-
-        whole = [(0, C)]
-        q3 = quantise("q3", round_weight("g3", raw3, 44), [(0, 128), (128, 256), (256, 512)])
 
         picked_ee = []
 
-        def ee_stage(t):
-            acc = edge_product(q3, t)
-            ee = keep.tile([P, S], F32, name="ee%d" % t)
-            nc.scalar.copy(ee[:], acc[:])
+        def ee_stage(t, weight, tag):
+            ee = keep.tile([P, S], F32, name="ee%d" % t, tag=tag)
+            if t == 0:
+                for n, copy in enumerate((nc.vector.tensor_copy, nc.scalar.copy)):
+                    cols = slice(n * V, (n + 1) * V)
+                    acc = bank(6 + n, [P, V])
+                    product(acc[:], weight, x_codes[:, cols], x_plane[:, cols])
+                    copy(ee[:, cols], acc[:])
+            else:
+                nc.scalar.copy(ee[:], edge_product(weight, t - 1)[:])
             picked = keep.tile([P, 3, V], F32, name="picked_ee%d" % t)
             for d in range(3):
                 nc.vector.tensor_copy(picked[:, d, :], ee[:].indirect(nxt[d][:]))
             picked_ee.append(picked)
 
-        ee_stage(0)
-        ee_stage(1)
-        q1 = quantise("q1", round_weight("g1", raw1, P), whole)
-        ee_stage(2)
-        q2 = quantise("q2", round_weight("g2", raw2, P), whole)
-        ee_stage(3)
+        q3 = prepare_plain("g3_0", raw3[0][:]) + prepare_plain("g3_1", raw3[1][:])
+        ee_stage(0, q3[0], "ee0")
+        q3 = q3 + prepare_plain("g3_2", raw3[2][:])
+        ee_stage(1, q3[1], "raw3_256")
+        q1 = prepare_plain("g1_lo", raw1_lo[:])
+        ee_stage(2, q3[2], "raw1_lo")
+        q2 = prepare_plain("g2_lo", raw2_lo[:])
+        ee_stage(3, q3[3], "raw2_lo")
+        q1 = q1 + prepare_plain("g1_hi", raw1_hi[:])
 
-        pair_sum = keep.tile([P, PACK, V], F32, name="pair_sum")
-        third = keep.tile([P, PACK, V], F32, name="third")
+        z_first = [bank(6 + h, [P, 3 * P]) for h in range(2)]
 
-        def a_stage(t):
-            acc1 = edge_product(q1, t)
-            acc2 = edge_product(q2, t)
-            gate = keep.tile([P, S], F32, name="gate%d" % t)
-            nc.scalar.activation(gate[:], acc1[:], SIGMOID)
-            a = keep.tile([P, S], F32, name="a%d" % t)
-            nc.vector.tensor_tensor(a[:], acc2[:], gate[:], MULT)
-            terms = keep.tile([P, 2, V], F32, name="terms%d" % t)
+        def make_a(first, tag):
+            gates = keep.tile([P, 2, S], F32, name="gates%d" % first, tag=tag)
+            made = []
+            for n in range(2):
+                acc1 = edge_product(q1[first + n], (3, 5, 1, 3)[first + n])
+                acc2 = edge_product(q2[first + n], (4, 0, 2, 4)[first + n])
+                nc.scalar.activation(gates[:, n, :], acc1[:], SIGMOID)
+                a = keep.tile([P, S], F32, name="a%d" % (first + n))
+                nc.vector.tensor_tensor(a[:], acc2[:], gates[:, n, :], MULT)
+                made.append(a)
+            return made
+
+        def add_terms(a, picked, terms, lo, hi, sums):
             for d in range(3):
-                dst = terms[:, d, :] if d < 2 else third[:, t, :]
-                nc.vector.tensor_tensor(dst, a[:].indirect(pos[d][:]), picked_ee[t][:, d, :], MULT)
-            nc.vector.tensor_tensor(pair_sum[:, t, :], terms[:, 0, :], terms[:, 1, :], ADD)
+                nc.vector.tensor_tensor(
+                    terms[:, d, lo:hi], a[:].indirect(pos[d][:, lo // 16 : hi // 16]), picked[:, d, lo:hi], MULT
+                )
+            for n, turned in enumerate(sums):
+                cols = slice(lo + n * HALF, lo + (n + 1) * HALF)
+                for d in range(3):
+                    nc.tensor.matmul(
+                        turned, terms[:, d, cols], identity[:], start=(d == 0), stop=(d == 2), is_transpose=True
+                    )
 
-        a_stage(0)
-        q5 = quantise("q5", round_weight("g5", raw5, P), whole)
-        a_stage(1)
-        q4 = quantise("q4", round_weight("g4", raw4, P), whole)
-        a_stage(2)
-        a_stage(3)
+        def add_whole(t, a, tag):
+            terms = keep.tile([P, 3, V], F32, name="terms%d" % t, tag=tag, align_bytes=64)
+            add_terms(a, picked_ee[t], terms, 0, V, [z_first[h][:, t * P : (t + 1) * P] for h in range(2)])
+
+        a_lo = make_a(0, "raw1_hi")
+        add_whole(0, a_lo[0], "terms0")
+        q2 = q2 + prepare_plain("g2_hi", raw2_hi[:])
+        q5 = quantise_tiles("g5", prepare_dealt("g5", [raw5]))
+        add_whole(1, a_lo[1], "g5")
+        a_hi = make_a(2, "raw5")
+        g4 = prepare_dealt("g4", [raw4])
+        add_whole(2, a_hi[0], "terms2")
+        terms3 = keep.tile([P, 3, V], F32, name="terms3")
+        z_last = []
+        for h in range(2):
+            turned = bank((2, 4)[h], [P, P])
+            add_terms(a_hi[1], picked_ee[3], terms3, h * HALF, (h + 1) * HALF, [turned[:]])
+            z_last.append(turned)
+        q4 = quantise_tiles("g4", g4)
 
         picked_gg = keep.tile([P, PACK, V], F32, name="picked_gg")
-        for t in range(PACK):
-            acc = edge_product(q5, t)
-            logits = keep.tile([P, S], F32, name="logits%d" % t)
-            nc.scalar.copy(logits[:], acc[:])
-            nc.scalar.activation(picked_gg[:, t, :], logits[:].indirect(own_t[:]), SIGMOID)
+        logits = [shared.tile([P, S], F32, name="logits%d" % t, offset=4 * S * t) for t in range(PACK)]
+        for t in range(PACK + 1):
+            if t < PACK:
+                nc.scalar.copy(logits[t][:], edge_product(q5[t], (5, 0, 1, 3)[t])[:])
+            if t > 0:
+                nc.scalar.activation(picked_gg[:, t - 1, :], logits[t - 1][:].indirect(own_t[:]), SIGMOID)
 
-        def by_lines(ap, h):
-            return ap[:, :, h * HALF : (h + 1) * HALF].rearrange("p t (c i) -> p c t i", i=4)
+        pairs = [shared.tile([P, C], BF16, name="pairs%d" % h, offset=4 * S * 3 + 2 * C * h) for h in range(2)]
 
-        def interleaved(ap):
-            return ap.rearrange("p (c i t) -> p c t i", i=4, t=PACK)
+        def round_z(h, turned, lo, hi):
+            dst = pairs[h][:].rearrange("v (u p e) -> v u p e", u=2, e=2)[:, :, lo:hi, :]
+            nc.scalar.copy(dst, turned.rearrange("v (p u e) -> v u p e", u=2, e=2))
 
-        z_grouped = [keep.tile([P, PACK * HALF], BF16, name="z_grouped%d" % h, align_bytes=64) for h in range(2)]
         for h in range(2):
-            nc.vector.tensor_tensor(interleaved(z_grouped[h][:]), by_lines(pair_sum[:], h), by_lines(third[:], h), ADD)
-        qz = [quantise("qz%d" % h, z_grouped[h], [(0, HALF)]) for h in range(2)]
+            round_z(h, z_first[h][:], 0, 96)
+        qz = []
+        for h in range(2):
+            round_z(h, z_last[h][:], 96, P)
+            back = bank((5, 0)[h], [P, 2, HALF])
+            for u in range(2):
+                nc.tensor.transpose(back[:, u, :], pairs[h][:].bitcast(F32)[:, u * P : (u + 1) * P], identity[:])
+            z_grouped = keep.tile([P, PACK * HALF], BF16, name="z_grouped%d" % h, align_bytes=64)
+            nc.scalar.copy(
+                z_grouped[:].bitcast(F32).rearrange("p (v u) -> p v u", u=2), back[:].rearrange("p u v -> p v u")
+            )
+            qz.append(quantise("qz%d" % h, z_grouped[:]))
 
-        result = keep.tile([P, 2, PACK, HALF], F32, name="result")
-        out_grouped = keep.tile([P, PACK * V], BF16, name="out_grouped", align_bytes=64)
+        out_codes = keep.tile([P, V], U32, name="out_codes", align_bytes=64)
+        out_plane = keep.tile([P, V], U8, name="out_plane", align_bytes=64)
         out_rows = out_0.rearrange("(p t) v -> p t v", t=PACK)
+        out_words = out_1[0].rearrange("p n t -> p (n t)").bitcast(I32)
         for h in range(2):
             cols = slice(h * HALF, (h + 1) * HALF)
-            rr = psum.tile([P, S], F32, name="acc")
+            rr = bank((1, 3)[h], [P, PACK, HALF])
             for t in range(PACK):
-                product(rr[:, t * HALF : (t + 1) * HALF], q4, t, qz[h][0][:], qz[h][1][:])
-            nc.vector.tensor_tensor(
-                result[:, h], rr[:].rearrange("p (t v) -> p t v", t=PACK), picked_gg[:, :, cols], MULT
-            )
-            nc.sync.dma_start(out_rows[:, :, cols], result[:, h])
-            nc.scalar.copy(
-                interleaved(out_grouped[:, h * PACK * HALF : (h + 1) * PACK * HALF]),
-                result[:, h].rearrange("p t (c i) -> p c t i", i=4),
-            )
-        out_codes, out_plane = quantise("qo", out_grouped, [(0, HALF), (HALF, V)])
-        nc.sync.dma_start(out_1[0].rearrange("p n t -> p (n t)").bitcast(I32), out_codes[:].bitcast(I32))
+                product(rr[:, t, :], q4[t], qz[h][0][:], qz[h][1][:])
+            result = keep.tile([P, PACK, HALF], F32, name="result%d" % h)
+            out_grouped = keep.tile([P, PACK * HALF], BF16, name="out_grouped%d" % h, align_bytes=64)
+            if h == 1:
+                nc.vector.tensor_tensor(interleaved(out_grouped[:]), by_lines(rr[:]), by_lines(picked_gg[:, :, cols]), MULT)
+            nc.vector.tensor_tensor(result[:], rr[:], picked_gg[:, :, cols], MULT)
+            nc.sync.dma_start(out_rows[:, :, cols], result[:])
+            if h == 0:
+                nc.scalar.copy(interleaved(out_grouped[:]), by_lines(result[:]))
+            nc.vector.quantize_mx(out=out_codes[:, cols].bitcast(FP8X4), scales=out_plane[:, cols], in_=out_grouped[:])
+            nc.sync.dma_start(out_words[:, cols], out_codes[:, cols].bitcast(I32))
         for q in range(4):
             queue = nc.scalar if q % 2 else nc.sync
             queue.dma_start(out_2[0, 4 * q : 4 * q + 4, :].bitcast(I32), out_plane[32 * q : 32 * q + 4, :].bitcast(I32))

@@ -53,7 +53,7 @@ def tile_picked_ytri_gated_po_kernel(
         offs_t = load_list("offs_t", offs)
         table_words = keep.tile([P, T], I32, name="table_words", align_bytes=64)
         nc.sync.dma_start(table_words[:], x_words[0].rearrange("p n t -> p (n t)").bitcast(I32))
-        raw3 = [load_weight("raw3_%d" % lo, w3, lo, hi) for lo, hi in ((0, 128), (128, 256), (256, 512))]
+        raw3 = [load_weight("raw3_%d" % lo, w3, lo, hi) for lo, hi in ((0, 128), (128, 256), (256, 384), (384, 512))]
         nxt = [load_list("nxt%d_t" % d, src) for d, src in enumerate((nxt1, nxt2, nxt3))]
         raw1_lo = load_weight("raw1_lo", w1, 0, V)
         raw2_lo = load_weight("raw2_lo", w2, 0, V)
@@ -62,8 +62,9 @@ def tile_picked_ytri_gated_po_kernel(
         raw2_hi = load_weight("raw2_hi", w2, V, C)
         raw5 = load_weight("raw5", w5, 0, C)
         own_t = load_list("own_t", own)
-        raw4 = shared.tile([P, PACK, C], F32, name="raw4", offset=0)
-        nc.sync.dma_start(raw4[:], w4.rearrange("(p j) c -> p j c", j=PACK))
+        raw4_lo = shared.tile([P, PACK, 384], F32, name="raw4_lo", offset=0)
+        nc.sync.dma_start(raw4_lo[:], w4.rearrange("(p j) c -> p j c", j=PACK)[:, :, :384])
+        raw4_hi = load_weight("raw4_hi", w4, 384, C)
 
         identity = keep.tile([P, P], F32, name="identity")
         make_identity(nc, identity[:])
@@ -92,15 +93,10 @@ def tile_picked_ytri_gated_po_kernel(
             codes, plane = quantise(name, grouped[:])
             return [(codes[:, lo : lo + P], plane[:, lo : lo + P]) for lo in range(0, raw.shape[2], P)]
 
-        def prepare_dealt(name, raws):
-            grouped = keep.tile([P, PACK * C], BF16, name=name, align_bytes=64)
+        def deal(copy, grouped, raw, first):
             dealt = grouped[:].rearrange("p (t m j) -> p m j t", t=PACK, j=PACK)
-            done = 0
-            for raw in raws:
-                count = raw.shape[2] // PACK
-                nc.scalar.copy(dealt[:, done : done + count], raw[:].rearrange("p j (m t) -> p m j t", t=PACK))
-                done = done + count
-            return grouped
+            count = raw.shape[2] // PACK
+            copy(dealt[:, first : first + count], raw[:].rearrange("p j (m t) -> p m j t", t=PACK))
 
         def quantise_tiles(name, grouped):
             codes, plane = quantise(name, grouped[:])
@@ -143,6 +139,7 @@ def tile_picked_ytri_gated_po_kernel(
         ee_stage(0, q3[0], "ee0")
         q3 = q3 + prepare_plain("g3_2", raw3[2][:])
         ee_stage(1, q3[1], "raw3_256")
+        q3 = q3 + prepare_plain("g3_3", raw3[3][:])
         q1 = prepare_plain("g1_lo", raw1_lo[:])
         ee_stage(2, q3[2], "raw1_lo")
         q2 = prepare_plain("g2_lo", raw2_lo[:])
@@ -182,10 +179,13 @@ def tile_picked_ytri_gated_po_kernel(
         a_lo = make_a(0, "raw1_hi")
         add_whole(0, a_lo[0], "terms0")
         q2 = q2 + prepare_plain("g2_hi", raw2_hi[:])
-        q5 = quantise_tiles("g5", prepare_dealt("g5", [raw5]))
+        g5 = keep.tile([P, PACK * C], BF16, name="g5", align_bytes=64)
+        deal(nc.scalar.copy, g5, raw5, 0)
+        q5 = quantise_tiles("g5", g5)
         add_whole(1, a_lo[1], "g5")
         a_hi = make_a(2, "raw5")
-        g4 = prepare_dealt("g4", [raw4])
+        g4 = keep.tile([P, PACK * C], BF16, name="g4", align_bytes=64)
+        deal(nc.scalar.copy, g4, raw4_lo, 0)
         add_whole(2, a_hi[0], "terms2")
         terms3 = keep.tile([P, 3, V], F32, name="terms3")
         z_last = []
@@ -193,17 +193,18 @@ def tile_picked_ytri_gated_po_kernel(
             turned = bank((2, 4)[h], [P, P])
             add_terms(a_hi[1], picked_ee[3], terms3, h * HALF, (h + 1) * HALF, [turned[:]])
             z_last.append(turned)
+        deal(nc.vector.tensor_copy, g4, raw4_hi, 384 // PACK)
         q4 = quantise_tiles("g4", g4)
 
         picked_gg = keep.tile([P, PACK, V], F32, name="picked_gg")
-        logits = [shared.tile([P, S], F32, name="logits%d" % t, offset=4 * S * t) for t in range(PACK)]
+        logits = [shared.tile([P, S], F32, name="logits%d" % t, offset=4 * S * (t % 2)) for t in range(PACK)]
         for t in range(PACK + 1):
             if t < PACK:
                 nc.scalar.copy(logits[t][:], edge_product(q5[t], (5, 0, 1, 3)[t])[:])
             if t > 0:
                 nc.scalar.activation(picked_gg[:, t - 1, :], logits[t - 1][:].indirect(own_t[:]), SIGMOID)
 
-        pairs = [shared.tile([P, C], BF16, name="pairs%d" % h, offset=4 * S * 3 + 2 * C * h) for h in range(2)]
+        pairs = [shared.tile([P, C], BF16, name="pairs%d" % h, offset=4 * S + 2 * C * h) for h in range(2)]
 
         def round_z(h, turned, lo, hi):
             dst = pairs[h][:].rearrange("v (u p e) -> v u p e", u=2, e=2)[:, :, lo:hi, :]
@@ -234,14 +235,14 @@ def tile_picked_ytri_gated_po_kernel(
                 product(rr[:, t, :], q4[t], qz[h][0][:], qz[h][1][:])
             result = keep.tile([P, PACK, HALF], F32, name="result%d" % h)
             out_grouped = keep.tile([P, PACK * HALF], BF16, name="out_grouped%d" % h, align_bytes=64)
-            if h == 1:
-                nc.vector.tensor_tensor(interleaved(out_grouped[:]), by_lines(rr[:]), by_lines(picked_gg[:, :, cols]), MULT)
             nc.vector.tensor_tensor(result[:], rr[:], picked_gg[:, :, cols], MULT)
             nc.sync.dma_start(out_rows[:, :, cols], result[:])
             if h == 0:
                 nc.scalar.copy(interleaved(out_grouped[:]), by_lines(result[:]))
+            else:
+                nc.vector.tensor_tensor(interleaved(out_grouped[:]), by_lines(rr[:]), by_lines(picked_gg[:, :, cols]), MULT)
             nc.vector.quantize_mx(out=out_codes[:, cols].bitcast(FP8X4), scales=out_plane[:, cols], in_=out_grouped[:])
-            nc.sync.dma_start(out_words[:, cols], out_codes[:, cols].bitcast(I32))
+            nc.scalar.dma_start(out_words[:, cols], out_codes[:, cols].bitcast(I32))
         for q in range(4):
             queue = nc.scalar if q % 2 else nc.sync
             queue.dma_start(out_2[0, 4 * q : 4 * q + 4, :].bitcast(I32), out_plane[32 * q : 32 * q + 4, :].bitcast(I32))

from contextlib import ExitStack

import concourse.mybir as mybir
from concourse.masks import make_identity

F32 = mybir.dt.float32
BF16 = mybir.dt.bfloat16
I32 = mybir.dt.int32
U32 = mybir.dt.uint32
U16 = mybir.dt.uint16
U8 = mybir.dt.uint8
FP8X4 = mybir.dt.float8_e4m3fn_x4
MULT = mybir.AluOpType.mult
SIGMOID = mybir.ActivationFunctionType.Sigmoid

P = 128
PACK = 4
T, S, V, C = 1024, 512, 256, 512
HALF = V // 2
FLOPS = 1207959552


def tile_picked_ytri_gated_po_kernel(
    tc, x_words, x_scales, w1, w2, w3, w4, w5, offs, pos1, pos2, pos3, nxt1, nxt2, nxt3, own, out_0, out_1, out_2
):
    nc = tc.nc
    with ExitStack() as ctx:
        keep = ctx.enter_context(tc.tile_pool(name="keep", bufs=1))
        shared = ctx.enter_context(tc.tile_pool(name="shared", bufs=1))
        psum = ctx.enter_context(tc.psum_pool(name="psum", bufs=1))

        def bank(n, shape):
            return psum.tile(shape, F32, name="acc", tag="bank%d" % n)

        def load_list(name, src):
            tile = keep.tile(list(src.shape), U16, name=name)
            nc.sync.dma_start(tile[:], src)
            return tile

        def load_weight(name, src, lo, hi):
            raw = keep.tile([P, PACK, hi - lo], F32, name=name)
            nc.sync.dma_start(raw[:], src.rearrange("(p j) c -> p j c", j=PACK)[:, :, lo:hi])
            return raw

        table_scales = keep.tile([P, T], U8, name="table_scales", align_bytes=64)
        for q in range(4):
            rows = x_scales[0, 4 * q : 4 * q + 4, :].bitcast(I32).rearrange("r c -> (r c)")
            nc.scalar.dma_start(table_scales[32 * q : 32 * q + 32, :].bitcast(I32), rows.partition_broadcast(8))
        warm = keep.tile([P, 2], F32, name="warm")
        nc.gpsimd.memset(warm[:, 0:1], 0.0)
        nc.scalar.activation(warm[:, 1:2], warm[:, 0:1], SIGMOID)

        offs_t = load_list("offs_t", offs)
        table_words = keep.tile([P, T], I32, name="table_words", align_bytes=64)
        nc.sync.dma_start(table_words[:], x_words[0].rearrange("p n t -> p (n t)").bitcast(I32))
        raw3 = [load_weight("raw3_%d" % lo, w3, lo, hi) for lo, hi in ((0, 128), (128, 256), (256, 384), (384, 512))]
        nxt = [load_list("nxt%d_t" % d, src) for d, src in enumerate((nxt1, nxt2, nxt3))]
        raw1_lo = load_weight("raw1_lo", w1, 0, V)
        raw2_lo = load_weight("raw2_lo", w2, 0, V)
        pos = [load_list("pos%d_t" % d, src) for d, src in enumerate((pos1, pos2, pos3))]
        raw1_hi = load_weight("raw1_hi", w1, V, C)
        raw2_hi = load_weight("raw2_hi", w2, V, C)
        raw5 = load_weight("raw5", w5, 0, C)
        own_t = load_list("own_t", own)
        raw4_lo = shared.tile([P, PACK, 384], F32, name="raw4_lo", offset=0)
        nc.sync.dma_start(raw4_lo[:], w4.rearrange("(p j) c -> p j c", j=PACK)[:, :, :384])
        raw4_hi = load_weight("raw4_hi", w4, 384, C)

        identity = keep.tile([P, P], F32, name="identity")
        make_identity(nc, identity[:])

        x_codes = keep.tile([P, S], I32, name="x_codes", align_bytes=64)
        x_plane = keep.tile([P, S], U8, name="x_plane", align_bytes=64)
        nc.vector.tensor_copy(x_plane[:], table_scales[:].indirect(offs_t[:]))
        nc.vector.tensor_copy(x_codes[:].bitcast(U32), table_words[:].bitcast(U32).indirect(offs_t[:]))

        def by_lines(ap):
            return ap.rearrange("p t (c i) -> p c t i", i=4)

        def interleaved(ap):
            return ap.rearrange("p (c i t) -> p c t i", i=4, t=PACK)

        def quantise(name, grouped):
            width = grouped.shape[1] // PACK
            codes = keep.tile([P, width], U32, name=name + "_codes", align_bytes=64)
            plane = keep.tile([P, width], U8, name=name + "_plane", align_bytes=64)
            nc.vector.quantize_mx(out=codes[:].bitcast(FP8X4), scales=plane[:], in_=grouped)
            return codes, plane

        def prepare_plain(name, raw):
            grouped = keep.tile([P, PACK * raw.shape[2]], BF16, name=name, align_bytes=64)
            nc.scalar.copy(interleaved(grouped[:]), by_lines(raw))
            codes, plane = quantise(name, grouped[:])
            return [(codes[:, lo : lo + P], plane[:, lo : lo + P]) for lo in range(0, raw.shape[2], P)]

        def deal(copy, grouped, raw, first):
            dealt = grouped[:].rearrange("p (t m j) -> p m j t", t=PACK, j=PACK)
            count = raw.shape[2] // PACK
            copy(dealt[:, first : first + count], raw[:].rearrange("p j (m t) -> p m j t", t=PACK))

        def quantise_tiles(name, grouped):
            codes, plane = quantise(name, grouped[:])
            return [(codes[:, lo : lo + P], plane[:, lo : lo + P]) for lo in range(0, codes.shape[1], P)]

        def product(out, weight, codes, plane):
            nc.tensor.matmul_mx(
                out=out,
                lhsT=weight[0].bitcast(FP8X4),
                lhsT_scale=weight[1],
                rhs=codes.bitcast(FP8X4),
                rhs_scale=plane,
                start=True,
                stop=True,
            )

        def edge_product(weight, n):
            acc = bank(n, [P, S])
            product(acc[:], weight, x_codes[:], x_plane[:])
            return acc

        picked_ee = []

        def ee_stage(t, weight, tag):
            ee = keep.tile([P, S], F32, name="ee%d" % t, tag=tag)
            if t == 0:
                for n, copy in enumerate((nc.vector.tensor_copy, nc.scalar.copy)):
                    cols = slice(n * V, (n + 1) * V)
                    acc = bank(6 + n, [P, V])
                    product(acc[:], weight, x_codes[:, cols], x_plane[:, cols])
                    copy(ee[:, cols], acc[:])
            else:
                nc.scalar.copy(ee[:], edge_product(weight, t - 1)[:])
            picked = keep.tile([P, 3, V], F32, name="picked_ee%d" % t)
            for d in range(3):
                nc.vector.tensor_copy(picked[:, d, :], ee[:].indirect(nxt[d][:]))
            picked_ee.append(picked)

        q3 = prepare_plain("g3_0", raw3[0][:]) + prepare_plain("g3_1", raw3[1][:])
        ee_stage(0, q3[0], "ee0")
        q3 = q3 + prepare_plain("g3_2", raw3[2][:])
        ee_stage(1, q3[1], "raw3_256")
        q3 = q3 + prepare_plain("g3_3", raw3[3][:])
        q1 = prepare_plain("g1_lo", raw1_lo[:])
        ee_stage(2, q3[2], "raw1_lo")
        q2 = prepare_plain("g2_lo", raw2_lo[:])
        ee_stage(3, q3[3], "raw2_lo")
        q1 = q1 + prepare_plain("g1_hi", raw1_hi[:])

        z_first = [bank(6 + h, [P, 3 * P]) for h in range(2)]

        def make_a(first, tag):
            gates = keep.tile([P, 2, S], F32, name="gates%d" % first, tag=tag)
            made = []
            for n in range(2):
                acc1 = edge_product(q1[first + n], (3, 5, 1, 3)[first + n])
                acc2 = edge_product(q2[first + n], (4, 0, 2, 4)[first + n])
                nc.scalar.activation(gates[:, n, :], acc1[:], SIGMOID)
                a = keep.tile([P, S], F32, name="a%d" % (first + n))
                nc.vector.tensor_tensor(a[:], acc2[:], gates[:, n, :], MULT)
                made.append(a)
            return made

        def add_terms(a, picked, terms, lo, hi, sums):
            for d in range(3):
                nc.vector.tensor_tensor(
                    terms[:, d, lo:hi], a[:].indirect(pos[d][:, lo // 16 : hi // 16]), picked[:, d, lo:hi], MULT
                )
            for n, turned in enumerate(sums):
                cols = slice(lo + n * HALF, lo + (n + 1) * HALF)
                for d in range(3):
                    nc.tensor.matmul(
                        turned, terms[:, d, cols], identity[:], start=(d == 0), stop=(d == 2), is_transpose=True
                    )

        def add_whole(t, a, tag):
            terms = keep.tile([P, 3, V], F32, name="terms%d" % t, tag=tag, align_bytes=64)
            add_terms(a, picked_ee[t], terms, 0, V, [z_first[h][:, t * P : (t + 1) * P] for h in range(2)])

        a_lo = make_a(0, "raw1_hi")
        add_whole(0, a_lo[0], "terms0")
        q2 = q2 + prepare_plain("g2_hi", raw2_hi[:])
        g5 = keep.tile([P, PACK * C], BF16, name="g5", align_bytes=64)
        deal(nc.scalar.copy, g5, raw5, 0)
        q5 = quantise_tiles("g5", g5)
        add_whole(1, a_lo[1], "g5")
        a_hi = make_a(2, "raw5")
        g4 = keep.tile([P, PACK * C], BF16, name="g4", align_bytes=64)
        deal(nc.scalar.copy, g4, raw4_lo, 0)
        add_whole(2, a_hi[0], "terms2")
        terms3 = keep.tile([P, 3, V], F32, name="terms3")
        z_last = []
        for h in range(2):
            turned = bank((2, 4)[h], [P, P])
            add_terms(a_hi[1], picked_ee[3], terms3, h * HALF, (h + 1) * HALF, [turned[:]])
            z_last.append(turned)
        deal(nc.vector.tensor_copy, g4, raw4_hi, 384 // PACK)
        q4 = quantise_tiles("g4", g4)

        picked_gg = keep.tile([P, PACK, V], F32, name="picked_gg")
        logits = [shared.tile([P, S], F32, name="logits%d" % t, offset=4 * S * (t % 2)) for t in range(PACK)]
        for t in range(PACK + 1):
            if t < PACK:
                nc.scalar.copy(logits[t][:], edge_product(q5[t], (5, 0, 1, 3)[t])[:])
            if t > 0:
                nc.scalar.activation(picked_gg[:, t - 1, :], logits[t - 1][:].indirect(own_t[:]), SIGMOID)

        pairs = [shared.tile([P, C], BF16, name="pairs%d" % h, offset=4 * S + 2 * C * h) for h in range(2)]

        def round_z(h, turned, lo, hi):
            dst = pairs[h][:].rearrange("v (u p e) -> v u p e", u=2, e=2)[:, :, lo:hi, :]
            nc.scalar.copy(dst, turned.rearrange("v (p u e) -> v u p e", u=2, e=2))

        for h in range(2):
            round_z(h, z_first[h][:], 0, 96)
        qz = []
        for h in range(2):
            round_z(h, z_last[h][:], 96, P)
            back = bank((5, 0)[h], [P, 2, HALF])
            for u in range(2):
                nc.tensor.transpose(back[:, u, :], pairs[h][:].bitcast(F32)[:, u * P : (u + 1) * P], identity[:])
            z_grouped = keep.tile([P, PACK * HALF], BF16, name="z_grouped%d" % h, align_bytes=64)
            nc.scalar.copy(
                z_grouped[:].bitcast(F32).rearrange("p (v u) -> p v u", u=2), back[:].rearrange("p u v -> p v u")
            )
            qz.append(quantise("qz%d" % h, z_grouped[:]))

        out_codes = keep.tile([P, V], U32, name="out_codes", align_bytes=64)
        out_plane = keep.tile([P, V], U8, name="out_plane", align_bytes=64)
        out_rows = out_0.rearrange("(p t) v -> p t v", t=PACK)
        out_words = out_1[0].rearrange("p n t -> p (n t)").bitcast(I32)
        for h in range(2):
            cols = slice(h * HALF, (h + 1) * HALF)
            rr = bank((1, 3)[h], [P, PACK, HALF])
            for t in range(PACK):
                product(rr[:, t, :], q4[t], qz[h][0][:], qz[h][1][:])
            result = keep.tile([P, PACK, HALF], F32, name="result%d" % h)
            out_grouped = keep.tile([P, PACK * HALF], BF16, name="out_grouped%d" % h, align_bytes=64)
            nc.vector.tensor_tensor(result[:], rr[:], picked_gg[:, :, cols], MULT)
            nc.sync.dma_start(out_rows[:, :, cols], result[:])
            if h == 0:
                nc.scalar.copy(interleaved(out_grouped[:]), by_lines(result[:]))
            else:
                nc.vector.tensor_tensor(interleaved(out_grouped[:]), by_lines(rr[:]), by_lines(picked_gg[:, :, cols]), MULT)
            nc.vector.quantize_mx(out=out_codes[:, cols].bitcast(FP8X4), scales=out_plane[:, cols], in_=out_grouped[:])
            nc.scalar.dma_start(out_words[:, cols], out_codes[:, cols].bitcast(I32))
        for q in range(4):
            queue = nc.scalar if q % 2 else nc.sync
            queue.dma_start(out_2[0, 4 * q : 4 * q + 4, :].bitcast(I32), out_plane[32 * q : 32 * q + 4, :].bitcast(I32))
